import numpy as np
import ml_dtypes


def mxq(x, axis, fmt="e4m3"):
    dtype, down = {"e4m3": (ml_dtypes.float8_e4m3fn, 7), "e5m2": (ml_dtypes.float8_e5m2, 14)}[fmt]
    v = np.moveaxis(np.asarray(x, np.float32).astype(ml_dtypes.bfloat16).astype(np.float64), axis, -1)
    blocks = v.reshape(v.shape[:-1] + (-1, 32))
    amax = np.abs(blocks).max(-1, keepdims=True)
    byte = np.maximum(np.where(amax > 0, np.frexp(amax)[1] - 1 + 127, 0) - down, 1)
    scale = np.exp2(byte - 127.0)
    codes = (blocks / scale).astype(np.float32).astype(dtype).astype(np.float64)
    return np.moveaxis((codes * scale).reshape(v.shape), -1, axis)


WIDE = False


def mx_kscale(k):
    if not WIDE:
        return np.ones(k)
    levels = np.array([10, -10, 5, -5, 0])
    if k % 512:
        return np.exp2(np.random.permutation(np.resize(levels, k // 32))).repeat(32)
    a = np.empty((k // 512, 16))
    for p in range(k // 512):
        a[p, :8] = np.random.permutation(np.resize(levels, 8))
        for g in range(8):
            far = levels[np.abs(levels - a[p, g]) >= 10]
            a[p, g + 8] = far[np.random.randint(len(far))]
    return np.exp2(a.ravel()).repeat(32)


def f64(x):
    return np.asarray(x).astype(np.float64)


def striped(idx):
    return np.tile(np.asarray(idx).reshape(-1, 16).T, (8, 1)).astype(np.uint16)


def unstriped(offs):
    return offs[:16].T.reshape(-1).astype(np.int64)


E2M1 = np.array([0.0, 0.5, 1.0, 1.5, 2.0, 3.0, 4.0, 6.0, -0.0, -0.5, -1.0, -1.5, -2.0, -3.0, -4.0, -6.0])


def pack_weight(w, fmt):
    k, n = w.shape
    w = f64(np.asarray(w, np.float32).astype(ml_dtypes.bfloat16)).reshape(k // 32, 32, n)
    amax = np.abs(w).max(1)
    if fmt == "e4m3":
        byte = np.frexp(amax)[1] - 1 + 127 - 7
    else:
        mant, ex = np.frexp(amax / 6.0)
        byte = np.where(mant > 0.5, ex, ex - 1) + 127
    byte = np.clip(np.where(amax > 0, byte, 1), 1, 254)
    scaled = (w * np.exp2(127.0 - byte)[:, None, :]).reshape(k, n).astype(np.float32)
    by_word = np.ascontiguousarray(scaled.reshape(k // 512, 128, 4, n).transpose(0, 1, 3, 2))
    if fmt == "e4m3":
        words = by_word.astype(ml_dtypes.float8_e4m3fn).view(np.uint8)
    else:
        c = by_word.astype(ml_dtypes.float4_e2m1fn).view(np.uint8) & 0xF
        words = (c[..., 0::2] | (c[..., 1::2] << 4)).reshape(k // 512, 128, 2 * n)
    return np.ascontiguousarray(words), np.ascontiguousarray(byte.astype(np.uint8).reshape(k // 512, 16, n))


def unpack_weight(words, scales, fmt):
    g, _, n = scales.shape
    words = np.ascontiguousarray(words).reshape(g, 128, n, -1)
    if fmt == "e4m3":
        vals = words.view(ml_dtypes.float8_e4m3fn).astype(np.float64)
    else:
        nib = np.empty((g, 128, n, 4), np.uint8)
        nib[..., 0::2] = words & 0xF
        nib[..., 1::2] = words >> 4
        vals = E2M1[nib]
    vals = vals * np.repeat(np.exp2(scales.astype(np.float64) - 127.0), 8, axis=1)[..., None]
    return vals.transpose(0, 1, 3, 2).reshape(g * 512, n)


def bf(x):
    return np.asarray(x, np.float32).astype(ml_dtypes.bfloat16)


def planes(Y):
    r, m = Y.shape
    b = f64(bf(Y)).reshape(r // 32, 32, m)
    amax = np.abs(b).max(1)
    byte = np.clip(np.where(amax > 0, np.frexp(amax)[1] - 1 + 127 - 7, 1), 1, 254)
    codes = (b * np.exp2(127.0 - byte)[:, None, :]).reshape(r, m).astype(np.float32).astype(ml_dtypes.float8_e4m3fn).view(np.uint8)
    words = codes.reshape(r // 512, 128, 4, m).transpose(0, 1, 3, 2)
    return np.ascontiguousarray(words), np.ascontiguousarray(byte.astype(np.uint8).reshape(r // 512, 16, m))


K, I, L, S, T, N = 1024, 512, 512, 512, 512, 512


def setup_inputs():
    n = np.random.standard_normal
    idx = np.random.randint(0, I, T)
    idx2 = np.random.randint(0, S, T)
    fk = mx_kscale(K)
    fl = mx_kscale(L)
    xap = pack_weight(n((K, I)) / fk[:, None], "e2m1")
    wap = pack_weight(n((K, N)) * 1 / np.sqrt(K) * fk[:, None], "e4m3")
    wbp = pack_weight(n((L, N)) * 1 / np.sqrt(L) * fl[:, None], "e2m1")
    return {
        "xa_words": xap[0],
        "xa_scales": xap[1],
        "wa_words": wap[0],
        "wa_scales": wap[1],
        "xb": (n((L, S)) / fl[:, None]).astype(np.float32),
        "wb_words": wbp[0],
        "wb_scales": wbp[1],
        "res": (1.0 * n((N, T))).astype(np.float32),
        "offs": striped(idx),
        "offs2": striped(idx2),
    }


def reference(xa_words, xa_scales, wa_words, wa_scales, xb, wb_words, wb_scales, res, offs, offs2):
    idx = unstriped(offs)
    idx2 = unstriped(offs2)
    xau = unpack_weight(xa_words, xa_scales, "e2m1")
    wau = unpack_weight(wa_words, wa_scales, "e4m3")
    wbu = unpack_weight(wb_words, wb_scales, "e2m1")
    za = wau.T @ xau
    xbq = mxq(f64(xb), 0, "e4m3")
    zb = wbu.T @ xbq
    y = np.maximum(za[:, idx], zb[:, idx2]) - 0.25 * np.square(za[:, idx] - zb[:, idx2]) + 0.3 * f64(res)
    words, scales = planes(y)
    return y, words, scales

@@ -1,0 +1,270 @@
+from contextlib import ExitStack
+
+import concourse.mybir as mybir
+from concourse.masks import make_identity
+
+K, I, L, S, T, N = 1024, 512, 512, 512, 512, 512
+FLOPS = 2 * K * N * I + 2 * L * N * S
+
+F32 = mybir.dt.float32
+BF16 = mybir.dt.bfloat16
+I32 = mybir.dt.int32
+U32 = mybir.dt.uint32
+U16 = mybir.dt.uint16
+U8 = mybir.dt.uint8
+FP8X4 = mybir.dt.float8_e4m3fn_x4
+FP4X4 = mybir.dt.float4_e2m1fn_x4
+ALU = mybir.AluOpType
+ACT = mybir.ActivationFunctionType
+
+P = 128
+PACK = 4
+HALF = 256
+WINDOW = 704
+XB_VECTOR_COLS = 64
+Y_VECTOR_COLS = 160
+DIRECT_UNITS = 2
+LAG = 3
+BASE_LEAD = 3
+
+
+def deal_columns(engine, dealt, raw, line):
+    engine.tensor_copy(
+        out=dealt.rearrange("p (r c i) -> p c r i", r=PACK, i=line),
+        in_=raw.rearrange("p (c i r) -> p c r i", r=PACK, i=line),
+    )
+
+
+def interleave(copy, grouped, rows):
+    copy(
+        out=grouped.rearrange("p (c i) j -> p c j i", i=4),
+        in_=rows.rearrange("p j (c i) -> p c j i", i=4),
+    )
+
+
+def load_scales(queue, plane, scales):
+    for q in range(4):
+        queue.dma_start(
+            out=plane[32 * q : 32 * q + 4, :].bitcast(I32).rearrange("q (z c) -> q z c", z=scales.shape[0]),
+            in_=scales[:, 4 * q : 4 * q + 4, :].rearrange("z q c -> q z c").bitcast(I32),
+        )
+
+
+def tile_moe_combine_by_larger_pl_kernel(
+    tc, xa_words, xa_scales, wa_words, wa_scales, xb, wb_words, wb_scales, res, offs, offs2, out_0, out_1, out_2
+):
+    nc = tc.nc
+    with ExitStack() as ctx:
+        keep = ctx.enter_context(tc.tile_pool(name="keep", bufs=1))
+        ring = ctx.enter_context(tc.tile_pool(name="ring", bufs=4))
+        psum = ctx.enter_context(tc.psum_pool(name="psum", bufs=1))
+
+        list_a = keep.tile([P, T // 16], U16, name="list_a")
+        list_b = keep.tile([P, T // 16], U16, name="list_b")
+
+        wb_scale_raw = keep.tile([P, N], U8, align_bytes=64, name="wb_scale_raw")
+        wa_scale_raw = keep.tile([P, 2 * N], U8, align_bytes=64, name="wa_scale_raw", tag="later_b")
+        xa_scale = keep.tile([P, 2 * I], U8, align_bytes=64, name="xa_scale")
+        nc.gpsimd.memset(wb_scale_raw[:].bitcast(I32), 0)
+        nc.gpsimd.memset(wa_scale_raw[:].bitcast(I32), 0)
+        nc.gpsimd.memset(xa_scale[:].bitcast(I32), 0)
+
+        xb_rows = xb.rearrange("(p j) s -> p j s", j=PACK)
+        xb_raw = [keep.tile([P, PACK, HALF], F32, name=f"xb_raw{h}") for h in range(2)]
+        wb_raw = keep.tile([P, 2 * N], U8, align_bytes=64, name="wb_raw")
+        wa_raw = keep.tile([P, 2, N], I32, align_bytes=64, name="wa_raw")
+        xa = keep.tile([P, 2, 2 * I], U8, align_bytes=64, name="xa")
+        nc.sync.dma_start(out=xb_raw[0][:], in_=xb_rows[:, :, :HALF])
+        load_scales(nc.sync, wb_scale_raw, wb_scales)
+        nc.sync.dma_start(out=wb_raw[:].bitcast(I32), in_=wb_words[0].bitcast(I32))
+        nc.sync.dma_start(out=xb_raw[1][:], in_=xb_rows[:, :, HALF:])
+        nc.sync.dma_start(list_b[:], offs2)
+        nc.sync.dma_start(out=wa_raw[:], in_=wa_words.rearrange("z p n t -> p z (n t)").bitcast(I32))
+        load_scales(nc.sync, wa_scale_raw, wa_scales)
+        nc.sync.dma_start(out=xa[:].bitcast(I32), in_=xa_words.rearrange("z p c -> p z c").bitcast(I32))
+        load_scales(nc.sync, xa_scale, xa_scales)
+        nc.sync.dma_start(list_a[:], offs)
+        zb = [keep.tile([P, WINDOW], F32, name=f"zb{r}") for r in range(PACK)]
+        za = [keep.tile([P, I], F32, name=f"za{r}") for r in range(PACK)]
+        for r in range(PACK):
+            nc.gpsimd.memset(zb[r][:, S:WINDOW], 0.0)
+        ident = keep.tile([P, P], F32, name="ident")
+        make_identity(nc, ident[:])
+
+        wb_scale = keep.tile([P, N], U8, align_bytes=64, name="wb_scale")
+        wb = keep.tile([P, 2 * N], U8, align_bytes=64, name="wb")
+        grouped = [keep.tile([P, HALF, PACK], BF16, align_bytes=64, name=f"xb_grouped{h}") for h in range(2)]
+        codes = [keep.tile([P, HALF], U32, align_bytes=64, name=f"xb_codes{h}") for h in range(2)]
+        scale = [keep.tile([P, HALF], U8, align_bytes=64, name=f"xb_scale{h}") for h in range(2)]
+        for h in range(2):
+            if h == 1:
+                interleave(nc.vector.tensor_copy, grouped[h][:], xb_raw[h][:])
+            else:
+                interleave(nc.vector.tensor_copy, grouped[h][:, :XB_VECTOR_COLS, :], xb_raw[h][:, :, :XB_VECTOR_COLS])
+                interleave(nc.scalar.copy, grouped[h][:, XB_VECTOR_COLS:, :], xb_raw[h][:, :, XB_VECTOR_COLS:])
+                deal_columns(nc.vector, wb_scale[:], wb_scale_raw[:], 16)
+                deal_columns(nc.vector, wb[:].bitcast(U16), wb_raw[:].bitcast(U16), 8)
+            nc.vector.quantize_mx(
+                out=codes[h][:].bitcast(FP8X4), scales=scale[h][:], in_=grouped[h][:].rearrange("p c j -> p (c j)")
+            )
+        banks = [("wide", 3)] * 3 + [("gap_t", 2)] * 2 + [("rest", 3)] * 3
+        for h in range(2):
+            for r in range(PACK):
+                tag, bufs = banks[PACK * h + r]
+                acc = psum.tile([P, HALF], F32, tag=tag, bufs=bufs, name="acc_b")
+                nc.tensor.matmul_mx(
+                    out=acc[:],
+                    lhsT=wb[:, 2 * P * r : 2 * P * (r + 1)].bitcast(FP4X4),
+                    lhsT_scale=wb_scale[:, P * r : P * (r + 1)],
+                    rhs=codes[h][:].bitcast(FP8X4),
+                    rhs_scale=scale[h][:],
+                    start=True,
+                    stop=True,
+                )
+                copy = nc.vector.tensor_copy if (h, r) == (1, 0) else nc.scalar.copy
+                copy(out=zb[r][:, h * HALF : (h + 1) * HALF], in_=acc[:])
+
+        res_rows = res.rearrange("(p r) t -> p r t", r=PACK)
+        res_sb = []
+        for g in range(2):
+            pair = keep.tile([P, 2, T], F32, name=f"res{g}")
+            nc.sync.dma_start(out=pair[:], in_=res_rows[:, 2 * g : 2 * g + 2, :])
+            res_sb.extend([pair[:, 0, :], pair[:, 1, :]])
+
+        wa_scale = keep.tile([P, 2, N], U8, align_bytes=64, name="wa_scale")
+        wa = keep.tile([P, 2, N], I32, align_bytes=64, name="wa")
+        b_first = keep.tile([P, T], F32, name="b_first")
+        nc.vector.tensor_copy(b_first[:], zb[0][:].indirect(list_b[:]))
+        for z in range(2):
+            deal_columns(nc.vector, wa[:, z, :], wa_raw[:, z, :], 4)
+        for z in range(2):
+            deal_columns(nc.vector, wa_scale[:, z, :], wa_scale_raw[:, z * N : (z + 1) * N], 16)
+        b_later = keep.tile([P, (PACK - 1) * T], F32, align_bytes=64, name="b_later", tag="later_b")
+        b = [b_first[:]] + [b_later[:, T * r : T * (r + 1)] for r in range(PACK - 1)]
+        for r in range(1, PACK):
+            nc.vector.tensor_copy(b[r], zb[r][:].indirect(list_b[:]))
+        for r in range(PACK):
+            acc = psum.tile([P, I], F32, tag="wide", bufs=3, name="acc_a")
+            for z in range(2):
+                nc.tensor.matmul_mx(
+                    out=acc[:],
+                    lhsT=wa[:, z, P * r : P * (r + 1)].bitcast(FP8X4),
+                    lhsT_scale=wa_scale[:, z, P * r : P * (r + 1)],
+                    rhs=xa[:, z, :].bitcast(FP4X4),
+                    rhs_scale=xa_scale[:, z * I : (z + 1) * I],
+                    start=(z == 0),
+                    stop=(z == 1),
+                )
+            nc.scalar.copy(out=za[r][:], in_=acc[:])
+
+        y = [keep.tile([P, PACK, HALF], F32, name=f"y{h}") for h in range(2)]
+        y_codes = keep.tile([P, T], U32, align_bytes=64, name="y_codes")
+        y_scale = keep.tile([P, T], U8, align_bytes=64, name="y_scale")
+        out_rows = out_0.rearrange("(p r) t -> p r t", r=PACK)
+        words_out = out_1[0].rearrange("p c t -> p (c t)").bitcast(I32)
+        units = [(h, r) for h in range(2) for r in range(PACK)]
+        first_direct = len(units) - DIRECT_UNITS
+        bases, gaps, squares, rests, largers = {}, {}, {}, {}, {}
+
+        def turn(acc, source, start, stop):
+            for j in range(2):
+                cols = slice(P * j, P * (j + 1))
+                nc.tensor.matmul(acc[:, cols], source[:, cols], ident[:], start=start and j == 0, stop=stop and j == 1, is_transpose=True)
+
+        def base(u):
+            h, r = units[u]
+            cols = slice(h * HALF, (h + 1) * HALF)
+            scaled = ring.tile([P, HALF], F32, name="scaled")
+            nc.scalar.activation(scaled[:], res_sb[r][:, cols], ACT.Copy, scale=0.3)
+            acc = psum.tile([P, HALF], F32, tag="wide", bufs=3, name="acc_base")
+            turn(acc, b[r][:, cols], True, False)
+            turn(acc, scaled, False, True)
+            bases[u] = keep.tile([P, HALF], F32, name=f"neg_base_t{u}")
+            nc.scalar.activation(bases[u][:], acc[:], ACT.Copy, scale=-1.0)
+
+        def front(u):
+            h, r = units[u]
+            gap = ring.tile([P, HALF], F32, name="gap", bufs=4)
+            nc.vector.tensor_tensor(
+                gap[:],
+                za[r][:].indirect(list_a[:, h * HALF // 16 : (h + 1) * HALF // 16]),
+                b[r][:, h * HALF : (h + 1) * HALF],
+                ALU.subtract,
+            )
+            square = ring.tile([P, HALF], F32, name="square")
+            if u >= first_direct:
+                nc.scalar.activation(square[:], gap[:], ACT.Square, scale=0.5)
+            else:
+                gap_t = psum.tile([P, HALF], F32, tag="gap_t", bufs=2, name="gap_t")
+                turn(gap_t, gap, True, True)
+                nc.scalar.activation(square[:], gap_t[:], ACT.Square, scale=0.5)
+            gaps[u], squares[u] = gap, square
+
+        def middle(u):
+            rests[u] = psum.tile([P, HALF], F32, tag="rest", bufs=3, name="rest")
+            turn(rests[u], bases[u], True, u >= first_direct)
+            if u < first_direct:
+                turn(rests[u], squares[u], False, True)
+
+        def store(u):
+            h, r = units[u]
+            nc.sync.dma_start(out=out_rows[:, r, h * HALF : (h + 1) * HALF], in_=y[h][:, r, :])
+
+        def back(u):
+            h, r = units[u]
+            nc.vector.scalar_tensor_tensor(y[h][:, r, :], gaps[u][:], 0.0, rests[u][:], ALU.max, ALU.subtract)
+            store(u)
+
+        def direct_larger(u):
+            largers[u] = ring.tile([P, HALF], F32, name="larger")
+            nc.vector.scalar_tensor_tensor(largers[u][:], gaps[u][:], 0.0, rests[u][:], ALU.max, ALU.subtract)
+
+        def direct_back(u):
+            h, r = units[u]
+            nc.vector.tensor_tensor(y[h][:, r, :], largers[u][:], squares[u][:], ALU.subtract)
+            store(u)
+
+        grouped_y = [keep.tile([P, HALF, PACK], BF16, align_bytes=64, name=f"y_grouped{h}") for h in range(2)]
+
+        def planes(h):
+            cols = slice(h * HALF, (h + 1) * HALF)
+            nc.vector.quantize_mx(
+                out=y_codes[:, cols].bitcast(FP8X4),
+                scales=y_scale[:, cols],
+                in_=grouped_y[h][:].rearrange("p c j -> p (c j)"),
+            )
+            nc.sync.dma_start(out=words_out[:, cols], in_=y_codes[:, cols].bitcast(I32))
+
+        def round_first_half(piece):
+            cols = slice(64 * piece, 64 * (piece + 1))
+            interleave(nc.scalar.copy, grouped_y[0][:, cols, :], y[0][:, :, cols])
+
+        for u in range(BASE_LEAD):
+            base(u)
+        for u in range(len(units)):
+            front(u)
+            if u + BASE_LEAD < len(units):
+                base(u + BASE_LEAD)
+            if u >= 1:
+                middle(u - 1)
+            if u >= LAG:
+                back(u - LAG)
+            if u >= 6:
+                round_first_half(2 * (u - 6))
+                round_first_half(2 * (u - 6) + 1)
+        middle(7)
+        direct_larger(6)
+        back(5)
+        direct_larger(7)
+        direct_back(6)
+        direct_back(7)
+        planes(0)
+        interleave(nc.vector.tensor_copy, grouped_y[1][:, :Y_VECTOR_COLS, :], y[1][:, :, :Y_VECTOR_COLS])
+        interleave(nc.scalar.copy, grouped_y[1][:, Y_VECTOR_COLS:, :], y[1][:, :, Y_VECTOR_COLS:])
+        planes(1)
+        for q in range(4):
+            queue = nc.scalar if q % 2 else nc.sync
+            queue.dma_start(
+                out=out_2[0, 4 * q : 4 * q + 4, :].bitcast(I32),
+                in_=y_scale[32 * q : 32 * q + 4, :].bitcast(I32),
+            )

@@ -21,11 +21,10 @@ P = 128
 PACK = 4
 HALF = 256
 WINDOW = 704
-XB_VECTOR_COLS = 64
-Y_VECTOR_COLS = 160
+XB_VECTOR_COLS = (128, 128)
+Y_VECTOR_COLS = 128
 DIRECT_UNITS = 2
-LAG = 3
-BASE_LEAD = 3
+LAG = 4
 
 
 def deal_columns(engine, dealt, raw, line):
@@ -81,9 +80,14 @@ def tile_moe_combine_by_larger_pl_kernel(
         nc.sync.dma_start(list_b[:], offs2)
         nc.sync.dma_start(out=wa_raw[:], in_=wa_words.rearrange("z p n t -> p z (n t)").bitcast(I32))
         load_scales(nc.sync, wa_scale_raw, wa_scales)
+        res_rows = res.rearrange("(p r) t -> p r t", r=PACK)
+        res_sb = [keep.tile([P, PACK, HALF], F32, name=f"res{h}") for h in range(2)]
+        nc.sync.dma_start(out=res_sb[0][:], in_=res_rows[:, :, :HALF])
         nc.sync.dma_start(out=xa[:].bitcast(I32), in_=xa_words.rearrange("z p c -> p z c").bitcast(I32))
         load_scales(nc.sync, xa_scale, xa_scales)
         nc.sync.dma_start(list_a[:], offs)
+        nc.sync.dma_start(out=res_sb[1][:], in_=res_rows[:, :, HALF:])
+        bank = [psum.tile([P, 512], F32, name=f"bank{i}") for i in range(8)]
         zb = [keep.tile([P, WINDOW], F32, name=f"zb{r}") for r in range(PACK)]
         za = [keep.tile([P, I], F32, name=f"za{r}") for r in range(PACK)]
         for r in range(PACK):
@@ -93,43 +97,35 @@ def tile_moe_combine_by_larger_pl_kernel(
 
         wb_scale = keep.tile([P, N], U8, align_bytes=64, name="wb_scale")
         wb = keep.tile([P, 2 * N], U8, align_bytes=64, name="wb")
-        grouped = [keep.tile([P, HALF, PACK], BF16, align_bytes=64, name=f"xb_grouped{h}") for h in range(2)]
+        grouped = keep.tile([P, HALF, PACK], BF16, align_bytes=64, name="xb_grouped")
         codes = [keep.tile([P, HALF], U32, align_bytes=64, name=f"xb_codes{h}") for h in range(2)]
         scale = [keep.tile([P, HALF], U8, align_bytes=64, name=f"xb_scale{h}") for h in range(2)]
         for h in range(2):
-            if h == 1:
-                interleave(nc.vector.tensor_copy, grouped[h][:], xb_raw[h][:])
-            else:
-                interleave(nc.vector.tensor_copy, grouped[h][:, :XB_VECTOR_COLS, :], xb_raw[h][:, :, :XB_VECTOR_COLS])
-                interleave(nc.scalar.copy, grouped[h][:, XB_VECTOR_COLS:, :], xb_raw[h][:, :, XB_VECTOR_COLS:])
-                deal_columns(nc.vector, wb_scale[:], wb_scale_raw[:], 16)
+            split = XB_VECTOR_COLS[h]
+            interleave(nc.vector.tensor_copy, grouped[:, :split, :], xb_raw[h][:, :, :split])
+            interleave(nc.scalar.copy, grouped[:, split:, :], xb_raw[h][:, :, split:])
+            if h == 0:
                 deal_columns(nc.vector, wb[:].bitcast(U16), wb_raw[:].bitcast(U16), 8)
             nc.vector.quantize_mx(
-                out=codes[h][:].bitcast(FP8X4), scales=scale[h][:], in_=grouped[h][:].rearrange("p c j -> p (c j)")
+                out=codes[h][:].bitcast(FP8X4), scales=scale[h][:], in_=grouped[:].rearrange("p c j -> p (c j)")
             )
-        banks = [("wide", 3)] * 3 + [("gap_t", 2)] * 2 + [("rest", 3)] * 3
-        for h in range(2):
-            for r in range(PACK):
-                tag, bufs = banks[PACK * h + r]
-                acc = psum.tile([P, HALF], F32, tag=tag, bufs=bufs, name="acc_b")
-                nc.tensor.matmul_mx(
-                    out=acc[:],
-                    lhsT=wb[:, 2 * P * r : 2 * P * (r + 1)].bitcast(FP4X4),
-                    lhsT_scale=wb_scale[:, P * r : P * (r + 1)],
-                    rhs=codes[h][:].bitcast(FP8X4),
-                    rhs_scale=scale[h][:],
-                    start=True,
-                    stop=True,
-                )
-                copy = nc.vector.tensor_copy if (h, r) == (1, 0) else nc.scalar.copy
-                copy(out=zb[r][:, h * HALF : (h + 1) * HALF], in_=acc[:])
-
-        res_rows = res.rearrange("(p r) t -> p r t", r=PACK)
-        res_sb = []
-        for g in range(2):
-            pair = keep.tile([P, 2, T], F32, name=f"res{g}")
-            nc.sync.dma_start(out=pair[:], in_=res_rows[:, 2 * g : 2 * g + 2, :])
-            res_sb.extend([pair[:, 0, :], pair[:, 1, :]])
+            if h == 0:
+                deal_columns(nc.vector, wb_scale[:], wb_scale_raw[:], 16)
+        for h, r, i in ((0, 0, 4), (0, 1, 5), (1, 0, 6), (1, 1, 7), (0, 2, 6), (0, 3, 7), (1, 2, 4), (1, 3, 5)):
+            acc = bank[i][:, :HALF]
+            nc.tensor.matmul_mx(
+                out=acc,
+                lhsT=wb[:, 2 * P * r : 2 * P * (r + 1)].bitcast(FP4X4),
+                lhsT_scale=wb_scale[:, P * r : P * (r + 1)],
+                rhs=codes[h][:].bitcast(FP8X4),
+                rhs_scale=scale[h][:],
+                start=True,
+                stop=True,
+            )
+            if (h, r) == (1, 0):
+                nc.vector.tensor_scalar(zb[r][:, h * HALF : (h + 1) * HALF], acc, -1.0, None, ALU.mult)
+            else:
+                nc.scalar.activation(zb[r][:, h * HALF : (h + 1) * HALF], acc, ACT.Copy, scale=-1.0)
 
         wa_scale = keep.tile([P, 2, N], U8, align_bytes=64, name="wa_scale")
         wa = keep.tile([P, 2, N], I32, align_bytes=64, name="wa")
@@ -144,7 +140,7 @@ def tile_moe_combine_by_larger_pl_kernel(
         for r in range(1, PACK):
             nc.vector.tensor_copy(b[r], zb[r][:].indirect(list_b[:]))
         for r in range(PACK):
-            acc = psum.tile([P, I], F32, tag="wide", bufs=3, name="acc_a")
+            acc = bank[r]
             for z in range(2):
                 nc.tensor.matmul_mx(
                     out=acc[:],
@@ -164,47 +160,39 @@ def tile_moe_combine_by_larger_pl_kernel(
         words_out = out_1[0].rearrange("p c t -> p (c t)").bitcast(I32)
         units = [(h, r) for h in range(2) for r in range(PACK)]
         first_direct = len(units) - DIRECT_UNITS
-        bases, gaps, squares, rests, largers = {}, {}, {}, {}, {}
+        gaps, squares, largers = {}, {}, {}
 
         def turn(acc, source, start, stop):
             for j in range(2):
                 cols = slice(P * j, P * (j + 1))
                 nc.tensor.matmul(acc[:, cols], source[:, cols], ident[:], start=start and j == 0, stop=stop and j == 1, is_transpose=True)
 
-        def base(u):
+        scaled = [keep.tile([P, PACK, HALF], F32, name=f"scaled{h}") for h in range(2)]
+        direct_base = keep.tile([P, DIRECT_UNITS, HALF], F32, name="direct_base")
+
+        def open_sum(u):
             h, r = units[u]
-            cols = slice(h * HALF, (h + 1) * HALF)
-            scaled = ring.tile([P, HALF], F32, name="scaled")
-            nc.scalar.activation(scaled[:], res_sb[r][:, cols], ACT.Copy, scale=0.3)
-            acc = psum.tile([P, HALF], F32, tag="wide", bufs=3, name="acc_base")
-            turn(acc, b[r][:, cols], True, False)
-            turn(acc, scaled, False, True)
-            bases[u] = keep.tile([P, HALF], F32, name=f"neg_base_t{u}")
-            nc.scalar.activation(bases[u][:], acc[:], ACT.Copy, scale=-1.0)
+            turn(bank[u % 4], b[r][:, h * HALF : (h + 1) * HALF], True, False)
+            turn(bank[u % 4], scaled[h][:, r, :], False, False)
 
         def front(u):
             h, r = units[u]
-            gap = ring.tile([P, HALF], F32, name="gap", bufs=4)
+            gap = ring.tile([P, HALF], F32, name="gap", bufs=LAG + 1)
             nc.vector.tensor_tensor(
                 gap[:],
                 za[r][:].indirect(list_a[:, h * HALF // 16 : (h + 1) * HALF // 16]),
                 b[r][:, h * HALF : (h + 1) * HALF],
-                ALU.subtract,
+                ALU.add,
             )
             square = ring.tile([P, HALF], F32, name="square")
-            if u >= first_direct:
-                nc.scalar.activation(square[:], gap[:], ACT.Square, scale=0.5)
-            else:
-                gap_t = psum.tile([P, HALF], F32, tag="gap_t", bufs=2, name="gap_t")
-                turn(gap_t, gap, True, True)
-                nc.scalar.activation(square[:], gap_t[:], ACT.Square, scale=0.5)
+            nc.scalar.activation(square[:], gap[:], ACT.Square, scale=0.5)
             gaps[u], squares[u] = gap, square
 
         def middle(u):
-            rests[u] = psum.tile([P, HALF], F32, tag="rest", bufs=3, name="rest")
-            turn(rests[u], bases[u], True, u >= first_direct)
-            if u < first_direct:
-                turn(rests[u], squares[u], False, True)
+            turn(bank[u % 4], squares[u], False, True)
+            turned = ring.tile([P, HALF], F32, name="turned")
+            nc.scalar.copy(out=turned[:], in_=bank[u % 4][:, :HALF])
+            turn(bank[4 + u % 4], turned, True, True)
 
         def store(u):
             h, r = units[u]
@@ -212,12 +200,12 @@ def tile_moe_combine_by_larger_pl_kernel(
 
         def back(u):
             h, r = units[u]
-            nc.vector.scalar_tensor_tensor(y[h][:, r, :], gaps[u][:], 0.0, rests[u][:], ALU.max, ALU.subtract)
+            nc.vector.scalar_tensor_tensor(y[h][:, r, :], gaps[u][:], 0.0, bank[4 + u % 4][:, :HALF], ALU.max, ALU.subtract)
             store(u)
 
         def direct_larger(u):
             largers[u] = ring.tile([P, HALF], F32, name="larger")
-            nc.vector.scalar_tensor_tensor(largers[u][:], gaps[u][:], 0.0, rests[u][:], ALU.max, ALU.subtract)
+            nc.vector.scalar_tensor_tensor(largers[u][:], gaps[u][:], 0.0, direct_base[:, u - first_direct, :], ALU.max, ALU.add)
 
         def direct_back(u):
             h, r = units[u]
@@ -239,27 +227,38 @@ def tile_moe_combine_by_larger_pl_kernel(
             cols = slice(64 * piece, 64 * (piece + 1))
             interleave(nc.scalar.copy, grouped_y[0][:, cols, :], y[0][:, :, cols])
 
-        for u in range(BASE_LEAD):
-            base(u)
+        nc.scalar.activation(scaled[0][:], res_sb[0][:], ACT.Copy, scale=-0.3)
+        for u in range(4):
+            open_sum(u)
+        nc.scalar.activation(scaled[1][:, :2, :], res_sb[1][:, :2, :], ACT.Copy, scale=-0.3)
         for u in range(len(units)):
             front(u)
-            if u + BASE_LEAD < len(units):
-                base(u + BASE_LEAD)
-            if u >= 1:
-                middle(u - 1)
             if u >= LAG:
                 back(u - LAG)
-            if u >= 6:
-                round_first_half(2 * (u - 6))
-                round_first_half(2 * (u - 6) + 1)
-        middle(7)
+            if u < first_direct:
+                middle(u)
+            if u + 4 < first_direct:
+                open_sum(u + 4)
+            if u == first_direct - 1:
+                nc.vector.scalar_tensor_tensor(
+                    direct_base[:],
+                    res_sb[1][:, 2:, :],
+                    0.3,
+                    b_later[:, T:].rearrange("p (r t) -> p r t", r=2)[:, :, HALF:],
+                    ALU.mult,
+                    ALU.subtract,
+                )
+        for piece in range(4):
+            round_first_half(piece)
         direct_larger(6)
-        back(5)
-        direct_larger(7)
+        for u in range(len(units) - LAG, first_direct - 1):
+            back(u)
         direct_back(6)
+        direct_larger(7)
+        back(5)
         direct_back(7)
-        planes(0)
         interleave(nc.vector.tensor_copy, grouped_y[1][:, :Y_VECTOR_COLS, :], y[1][:, :, :Y_VECTOR_COLS])
+        planes(0)
         interleave(nc.scalar.copy, grouped_y[1][:, Y_VECTOR_COLS:, :], y[1][:, :, Y_VECTOR_COLS:])
         planes(1)
         for q in range(4):

@@ -19,12 +19,11 @@ ACT = mybir.ActivationFunctionType
 
 P = 128
 PACK = 4
+TURNED = 2
 HALF = 256
 WINDOW = 704
 XB_VECTOR_COLS = (128, 128)
-Y_VECTOR_COLS = 128
-DIRECT_UNITS = 2
-LAG = 4
+WINDOW_A = 544
 
 
 def deal_columns(engine, dealt, raw, line):
@@ -55,7 +54,6 @@ def tile_moe_combine_by_larger_pl_kernel(
     nc = tc.nc
     with ExitStack() as ctx:
         keep = ctx.enter_context(tc.tile_pool(name="keep", bufs=1))
-        ring = ctx.enter_context(tc.tile_pool(name="ring", bufs=4))
         psum = ctx.enter_context(tc.psum_pool(name="psum", bufs=1))
 
         list_a = keep.tile([P, T // 16], U16, name="list_a")
@@ -64,40 +62,43 @@ def tile_moe_combine_by_larger_pl_kernel(
         wb_scale_raw = keep.tile([P, N], U8, align_bytes=64, name="wb_scale_raw")
         wa_scale_raw = keep.tile([P, 2 * N], U8, align_bytes=64, name="wa_scale_raw", tag="later_b")
         xa_scale = keep.tile([P, 2 * I], U8, align_bytes=64, name="xa_scale")
-        nc.gpsimd.memset(wb_scale_raw[:].bitcast(I32), 0)
+        nc.vector.memset(wb_scale_raw[:].bitcast(I32), 0)
         nc.gpsimd.memset(wa_scale_raw[:].bitcast(I32), 0)
         nc.gpsimd.memset(xa_scale[:].bitcast(I32), 0)
 
         xb_rows = xb.rearrange("(p j) s -> p j s", j=PACK)
-        xb_raw = [keep.tile([P, PACK, HALF], F32, name=f"xb_raw{h}") for h in range(2)]
+        zb_all = keep.tile([P, (PACK - 1) * S + WINDOW], F32, name="zb_all")
+        xb_first = keep.tile([P, PACK, HALF], F32, name="xb_first")
+        xb_raw = [xb_first[:], zb_all[:, 2 * S : 4 * S].rearrange("p (j s) -> p j s", j=PACK)]
         wb_raw = keep.tile([P, 2 * N], U8, align_bytes=64, name="wb_raw")
         wa_raw = keep.tile([P, 2, N], I32, align_bytes=64, name="wa_raw")
         xa = keep.tile([P, 2, 2 * I], U8, align_bytes=64, name="xa")
-        nc.sync.dma_start(out=xb_raw[0][:], in_=xb_rows[:, :, :HALF])
+        nc.sync.dma_start(out=xb_raw[0], in_=xb_rows[:, :, :HALF])
         load_scales(nc.sync, wb_scale_raw, wb_scales)
         nc.sync.dma_start(out=wb_raw[:].bitcast(I32), in_=wb_words[0].bitcast(I32))
-        nc.sync.dma_start(out=xb_raw[1][:], in_=xb_rows[:, :, HALF:])
-        nc.sync.dma_start(list_b[:], offs2)
+        nc.sync.dma_start(out=xb_raw[1], in_=xb_rows[:, :, HALF:])
         nc.sync.dma_start(out=wa_raw[:], in_=wa_words.rearrange("z p n t -> p z (n t)").bitcast(I32))
+        nc.sync.dma_start(list_b[:], offs2)
         load_scales(nc.sync, wa_scale_raw, wa_scales)
         res_rows = res.rearrange("(p r) t -> p r t", r=PACK)
-        res_sb = [keep.tile([P, PACK, HALF], F32, name=f"res{h}") for h in range(2)]
-        nc.sync.dma_start(out=res_sb[0][:], in_=res_rows[:, :, :HALF])
+        res_pairs = [keep.tile([P, 2, T], F32, name=f"res{g}") for g in range(2)]
+        nc.sync.dma_start(out=res_pairs[0][:], in_=res_rows[:, :2, :])
+        nc.sync.dma_start(out=res_pairs[1][:], in_=res_rows[:, 2:, :])
         nc.sync.dma_start(out=xa[:].bitcast(I32), in_=xa_words.rearrange("z p c -> p z c").bitcast(I32))
         load_scales(nc.sync, xa_scale, xa_scales)
         nc.sync.dma_start(list_a[:], offs)
-        nc.sync.dma_start(out=res_sb[1][:], in_=res_rows[:, :, HALF:])
         bank = [psum.tile([P, 512], F32, name=f"bank{i}") for i in range(8)]
-        zb = [keep.tile([P, WINDOW], F32, name=f"zb{r}") for r in range(PACK)]
-        za = [keep.tile([P, I], F32, name=f"za{r}") for r in range(PACK)]
+        zb = [zb_all[:, (PACK - 1 - r) * S : (PACK - 1 - r) * S + WINDOW] for r in range(PACK)]
+        za = [keep.tile([P, WINDOW_A], F32, name=f"za{r}") for r in range(PACK)]
         for r in range(PACK):
-            nc.gpsimd.memset(zb[r][:, S:WINDOW], 0.0)
+            nc.gpsimd.memset(za[r][:, I:], 0.0)
+        nc.gpsimd.memset(zb_all[:, PACK * S :], 0.0)
         ident = keep.tile([P, P], F32, name="ident")
         make_identity(nc, ident[:])
 
         wb_scale = keep.tile([P, N], U8, align_bytes=64, name="wb_scale")
         wb = keep.tile([P, 2 * N], U8, align_bytes=64, name="wb")
-        grouped = keep.tile([P, HALF, PACK], BF16, align_bytes=64, name="xb_grouped")
+        grouped = keep.tile([P, HALF, PACK], BF16, align_bytes=64, name="xb_grouped", tag="grouped_then_wa")
         codes = [keep.tile([P, HALF], U32, align_bytes=64, name=f"xb_codes{h}") for h in range(2)]
         scale = [keep.tile([P, HALF], U8, align_bytes=64, name=f"xb_scale{h}") for h in range(2)]
         for h in range(2):
@@ -111,6 +112,9 @@ def tile_moe_combine_by_larger_pl_kernel(
             )
             if h == 0:
                 deal_columns(nc.vector, wb_scale[:], wb_scale_raw[:], 16)
+        wa = keep.tile([P, 2, N], I32, align_bytes=64, name="wa", tag="grouped_then_wa")
+        for z in range(2):
+            deal_columns(nc.vector, wa[:, z, :], wa_raw[:, z, :], 4)
         for h, r, i in ((0, 0, 4), (0, 1, 5), (1, 0, 6), (1, 1, 7), (0, 2, 6), (0, 3, 7), (1, 2, 4), (1, 3, 5)):
             acc = bank[i][:, :HALF]
             nc.tensor.matmul_mx(
@@ -128,17 +132,12 @@ def tile_moe_combine_by_larger_pl_kernel(
                 nc.scalar.activation(zb[r][:, h * HALF : (h + 1) * HALF], acc, ACT.Copy, scale=-1.0)
 
         wa_scale = keep.tile([P, 2, N], U8, align_bytes=64, name="wa_scale")
-        wa = keep.tile([P, 2, N], I32, align_bytes=64, name="wa")
-        b_first = keep.tile([P, T], F32, name="b_first")
-        nc.vector.tensor_copy(b_first[:], zb[0][:].indirect(list_b[:]))
-        for z in range(2):
-            deal_columns(nc.vector, wa[:, z, :], wa_raw[:, z, :], 4)
         for z in range(2):
             deal_columns(nc.vector, wa_scale[:, z, :], wa_scale_raw[:, z * N : (z + 1) * N], 16)
-        b_later = keep.tile([P, (PACK - 1) * T], F32, align_bytes=64, name="b_later", tag="later_b")
-        b = [b_first[:]] + [b_later[:, T * r : T * (r + 1)] for r in range(PACK - 1)]
-        for r in range(1, PACK):
-            nc.vector.tensor_copy(b[r], zb[r][:].indirect(list_b[:]))
+        b_all = keep.tile([P, PACK * T], F32, align_bytes=64, name="b_all", tag="later_b")
+        b = [b_all[:, T * r : T * (r + 1)] for r in range(PACK)]
+        for r in range(PACK):
+            nc.vector.tensor_copy(b[r], zb[r].indirect(list_b[:]))
         for r in range(PACK):
             acc = bank[r]
             for z in range(2):
@@ -151,116 +150,73 @@ def tile_moe_combine_by_larger_pl_kernel(
                     start=(z == 0),
                     stop=(z == 1),
                 )
-            nc.scalar.copy(out=za[r][:], in_=acc[:])
+            nc.scalar.copy(out=za[r][:, :I], in_=acc[:])
 
-        y = [keep.tile([P, PACK, HALF], F32, name=f"y{h}") for h in range(2)]
-        y_codes = keep.tile([P, T], U32, align_bytes=64, name="y_codes")
-        y_scale = keep.tile([P, T], U8, align_bytes=64, name="y_scale")
+        y = keep.tile([P, PACK, T], F32, name="y")
         out_rows = out_0.rearrange("(p r) t -> p r t", r=PACK)
-        words_out = out_1[0].rearrange("p c t -> p (c t)").bitcast(I32)
-        units = [(h, r) for h in range(2) for r in range(PACK)]
-        first_direct = len(units) - DIRECT_UNITS
-        gaps, squares, largers = {}, {}, {}
+        scaled = keep.tile([P, TURNED, T], F32, name="scaled")
+        nc.scalar.activation(scaled[:], res_pairs[0][:], ACT.Copy, scale=-0.3)
 
         def turn(acc, source, start, stop):
-            for j in range(2):
+            for j in range(T // P):
                 cols = slice(P * j, P * (j + 1))
-                nc.tensor.matmul(acc[:, cols], source[:, cols], ident[:], start=start and j == 0, stop=stop and j == 1, is_transpose=True)
+                nc.tensor.matmul(
+                    acc[:, cols],
+                    source[:, cols],
+                    ident[:],
+                    start=start and j == 0,
+                    stop=stop and j == T // P - 1,
+                    is_transpose=True,
+                )
 
-        scaled = [keep.tile([P, PACK, HALF], F32, name=f"scaled{h}") for h in range(2)]
-        direct_base = keep.tile([P, DIRECT_UNITS, HALF], F32, name="direct_base")
-
-        def open_sum(u):
-            h, r = units[u]
-            turn(bank[u % 4], b[r][:, h * HALF : (h + 1) * HALF], True, False)
-            turn(bank[u % 4], scaled[h][:, r, :], False, False)
-
-        def front(u):
-            h, r = units[u]
-            gap = ring.tile([P, HALF], F32, name="gap", bufs=LAG + 1)
-            nc.vector.tensor_tensor(
-                gap[:],
-                za[r][:].indirect(list_a[:, h * HALF // 16 : (h + 1) * HALF // 16]),
-                b[r][:, h * HALF : (h + 1) * HALF],
-                ALU.add,
-            )
-            square = ring.tile([P, HALF], F32, name="square")
+        for r in range(TURNED):
+            turn(bank[r], b[r], True, False)
+            turn(bank[r], scaled[:, r, :], False, False)
+        gaps, squares = [], []
+        for r in range(PACK):
+            gap = keep.tile([P, T], F32, name=f"gap{r}")
+            nc.vector.tensor_tensor(gap[:], za[r][:].indirect(list_a[:]), b[r], ALU.add)
+            square = keep.tile([P, T], F32, name=f"square{r}")
             nc.scalar.activation(square[:], gap[:], ACT.Square, scale=0.5)
-            gaps[u], squares[u] = gap, square
+            gaps.append(gap)
+            squares.append(square)
+            if r < TURNED:
+                turn(bank[r], square, False, True)
+                turned = keep.tile([P, T], F32, name=f"turned{r}")
+                nc.scalar.copy(out=turned[:], in_=bank[r][:])
+                turn(bank[PACK + r], turned, True, True)
 
-        def middle(u):
-            turn(bank[u % 4], squares[u], False, True)
-            turned = ring.tile([P, HALF], F32, name="turned")
-            nc.scalar.copy(out=turned[:], in_=bank[u % 4][:, :HALF])
-            turn(bank[4 + u % 4], turned, True, True)
+        def store(r, cols):
+            nc.sync.dma_start(out=out_rows[:, r, cols], in_=y[:, r, cols])
 
-        def store(u):
-            h, r = units[u]
-            nc.sync.dma_start(out=out_rows[:, r, h * HALF : (h + 1) * HALF], in_=y[h][:, r, :])
+        bases = [b[r - TURNED] for r in range(TURNED, PACK)]
+        largers = [keep.tile([P, T], F32, name=f"larger{r}") for r in range(TURNED, PACK)]
+        for i, r in enumerate(range(TURNED, PACK)):
+            nc.vector.scalar_tensor_tensor(bases[i], res_pairs[1][:, i, :], 0.3, b[r], ALU.mult, ALU.subtract)
+        for i, r in enumerate(range(TURNED, PACK)):
+            nc.vector.scalar_tensor_tensor(largers[i][:], gaps[r][:], 0.0, bases[i], ALU.max, ALU.add)
+        for i, r in enumerate(range(TURNED, PACK)):
+            nc.vector.tensor_tensor(y[:, r, :], largers[i][:], squares[r][:], ALU.subtract)
+            store(r, slice(0, T))
+        for r, cols in ((0, slice(0, T)), (1, slice(HALF, T)), (1, slice(0, HALF))):
+            nc.vector.scalar_tensor_tensor(
+                y[:, r, cols], gaps[r][:, cols], 0.0, bank[PACK + r][:, cols], ALU.max, ALU.subtract
+            )
+            store(r, cols)
 
-        def back(u):
-            h, r = units[u]
-            nc.vector.scalar_tensor_tensor(y[h][:, r, :], gaps[u][:], 0.0, bank[4 + u % 4][:, :HALF], ALU.max, ALU.subtract)
-            store(u)
-
-        def direct_larger(u):
-            largers[u] = ring.tile([P, HALF], F32, name="larger")
-            nc.vector.scalar_tensor_tensor(largers[u][:], gaps[u][:], 0.0, direct_base[:, u - first_direct, :], ALU.max, ALU.add)
-
-        def direct_back(u):
-            h, r = units[u]
-            nc.vector.tensor_tensor(y[h][:, r, :], largers[u][:], squares[u][:], ALU.subtract)
-            store(u)
-
-        grouped_y = [keep.tile([P, HALF, PACK], BF16, align_bytes=64, name=f"y_grouped{h}") for h in range(2)]
-
-        def planes(h):
+        y_codes = keep.tile([P, T], U32, align_bytes=64, name="y_codes")
+        y_scale = keep.tile([P, T], U8, align_bytes=64, name="y_scale")
+        words_out = out_1[0].rearrange("p c t -> p (c t)").bitcast(I32)
+        for h, copy in ((0, nc.vector.tensor_copy), (1, nc.scalar.copy)):
             cols = slice(h * HALF, (h + 1) * HALF)
+            grouped_y = keep.tile([P, HALF, PACK], BF16, align_bytes=64, name=f"y_grouped{h}")
+            interleave(copy, grouped_y[:], y[:, :, cols])
             nc.vector.quantize_mx(
                 out=y_codes[:, cols].bitcast(FP8X4),
                 scales=y_scale[:, cols],
-                in_=grouped_y[h][:].rearrange("p c j -> p (c j)"),
+                in_=grouped_y[:].rearrange("p c j -> p (c j)"),
             )
             nc.sync.dma_start(out=words_out[:, cols], in_=y_codes[:, cols].bitcast(I32))
-
-        def round_first_half(piece):
-            cols = slice(64 * piece, 64 * (piece + 1))
-            interleave(nc.scalar.copy, grouped_y[0][:, cols, :], y[0][:, :, cols])
-
-        nc.scalar.activation(scaled[0][:], res_sb[0][:], ACT.Copy, scale=-0.3)
-        for u in range(4):
-            open_sum(u)
-        nc.scalar.activation(scaled[1][:, :2, :], res_sb[1][:, :2, :], ACT.Copy, scale=-0.3)
-        for u in range(len(units)):
-            front(u)
-            if u >= LAG:
-                back(u - LAG)
-            if u < first_direct:
-                middle(u)
-            if u + 4 < first_direct:
-                open_sum(u + 4)
-            if u == first_direct - 1:
-                nc.vector.scalar_tensor_tensor(
-                    direct_base[:],
-                    res_sb[1][:, 2:, :],
-                    0.3,
-                    b_later[:, T:].rearrange("p (r t) -> p r t", r=2)[:, :, HALF:],
-                    ALU.mult,
-                    ALU.subtract,
-                )
-        for piece in range(4):
-            round_first_half(piece)
-        direct_larger(6)
-        for u in range(len(units) - LAG, first_direct - 1):
-            back(u)
-        direct_back(6)
-        direct_larger(7)
-        back(5)
-        direct_back(7)
-        interleave(nc.vector.tensor_copy, grouped_y[1][:, :Y_VECTOR_COLS, :], y[1][:, :, :Y_VECTOR_COLS])
-        planes(0)
-        interleave(nc.scalar.copy, grouped_y[1][:, Y_VECTOR_COLS:, :], y[1][:, :, Y_VECTOR_COLS:])
-        planes(1)
         for q in range(4):
             queue = nc.scalar if q % 2 else nc.sync
             queue.dma_start(

from contextlib import ExitStack

import concourse.mybir as mybir
from concourse.masks import make_identity

K, I, L, S, T, N = 1024, 512, 512, 512, 512, 512
FLOPS = 2 * K * N * I + 2 * L * N * S

F32 = mybir.dt.float32
BF16 = mybir.dt.bfloat16
I32 = mybir.dt.int32
U32 = mybir.dt.uint32
U16 = mybir.dt.uint16
U8 = mybir.dt.uint8
FP8X4 = mybir.dt.float8_e4m3fn_x4
FP4X4 = mybir.dt.float4_e2m1fn_x4
ALU = mybir.AluOpType
ACT = mybir.ActivationFunctionType

P = 128
PACK = 4
TURNED = 2
HALF = 256
WINDOW = 704
XB_VECTOR_COLS = (128, 128)
WINDOW_A = 544


def deal_columns(engine, dealt, raw, line):
    engine.tensor_copy(
        out=dealt.rearrange("p (r c i) -> p c r i", r=PACK, i=line),
        in_=raw.rearrange("p (c i r) -> p c r i", r=PACK, i=line),
    )


def interleave(copy, grouped, rows):
    copy(
        out=grouped.rearrange("p (c i) j -> p c j i", i=4),
        in_=rows.rearrange("p j (c i) -> p c j i", i=4),
    )


def load_scales(queue, plane, scales):
    for q in range(4):
        queue.dma_start(
            out=plane[32 * q : 32 * q + 4, :].bitcast(I32).rearrange("q (z c) -> q z c", z=scales.shape[0]),
            in_=scales[:, 4 * q : 4 * q + 4, :].rearrange("z q c -> q z c").bitcast(I32),
        )


def tile_moe_combine_by_larger_pl_kernel(
    tc, xa_words, xa_scales, wa_words, wa_scales, xb, wb_words, wb_scales, res, offs, offs2, out_0, out_1, out_2
):
    nc = tc.nc
    with ExitStack() as ctx:
        keep = ctx.enter_context(tc.tile_pool(name="keep", bufs=1))
        psum = ctx.enter_context(tc.psum_pool(name="psum", bufs=1))

        list_a = keep.tile([P, T // 16], U16, name="list_a")
        list_b = keep.tile([P, T // 16], U16, name="list_b")

        wb_scale_raw = keep.tile([P, N], U8, align_bytes=64, name="wb_scale_raw")
        wa_scale_raw = keep.tile([P, 2 * N], U8, align_bytes=64, name="wa_scale_raw", tag="later_b")
        xa_scale = keep.tile([P, 2 * I], U8, align_bytes=64, name="xa_scale")
        nc.vector.memset(wb_scale_raw[:].bitcast(I32), 0)
        nc.gpsimd.memset(wa_scale_raw[:].bitcast(I32), 0)
        nc.gpsimd.memset(xa_scale[:].bitcast(I32), 0)

        xb_rows = xb.rearrange("(p j) s -> p j s", j=PACK)
        zb_all = keep.tile([P, (PACK - 1) * S + WINDOW], F32, name="zb_all")
        xb_first = keep.tile([P, PACK, HALF], F32, name="xb_first")
        xb_raw = [xb_first[:], zb_all[:, 2 * S : 4 * S].rearrange("p (j s) -> p j s", j=PACK)]
        wb_raw = keep.tile([P, 2 * N], U8, align_bytes=64, name="wb_raw")
        wa_raw = keep.tile([P, 2, N], I32, align_bytes=64, name="wa_raw")
        xa = keep.tile([P, 2, 2 * I], U8, align_bytes=64, name="xa")
        nc.sync.dma_start(out=xb_raw[0], in_=xb_rows[:, :, :HALF])
        load_scales(nc.sync, wb_scale_raw, wb_scales)
        nc.sync.dma_start(out=wb_raw[:].bitcast(I32), in_=wb_words[0].bitcast(I32))
        nc.sync.dma_start(out=xb_raw[1], in_=xb_rows[:, :, HALF:])
        nc.sync.dma_start(out=wa_raw[:], in_=wa_words.rearrange("z p n t -> p z (n t)").bitcast(I32))
        nc.sync.dma_start(list_b[:], offs2)
        load_scales(nc.sync, wa_scale_raw, wa_scales)
        res_rows = res.rearrange("(p r) t -> p r t", r=PACK)
        res_pairs = [keep.tile([P, 2, T], F32, name=f"res{g}") for g in range(2)]
        nc.sync.dma_start(out=res_pairs[0][:], in_=res_rows[:, :2, :])
        nc.sync.dma_start(out=res_pairs[1][:], in_=res_rows[:, 2:, :])
        nc.sync.dma_start(out=xa[:].bitcast(I32), in_=xa_words.rearrange("z p c -> p z c").bitcast(I32))
        load_scales(nc.sync, xa_scale, xa_scales)
        nc.sync.dma_start(list_a[:], offs)
        bank = [psum.tile([P, 512], F32, name=f"bank{i}") for i in range(8)]
        zb = [zb_all[:, (PACK - 1 - r) * S : (PACK - 1 - r) * S + WINDOW] for r in range(PACK)]
        za = [keep.tile([P, WINDOW_A], F32, name=f"za{r}") for r in range(PACK)]
        for r in range(PACK):
            nc.gpsimd.memset(za[r][:, I:], 0.0)
        nc.gpsimd.memset(zb_all[:, PACK * S :], 0.0)
        ident = keep.tile([P, P], F32, name="ident")
        make_identity(nc, ident[:])

        wb_scale = keep.tile([P, N], U8, align_bytes=64, name="wb_scale")
        wb = keep.tile([P, 2 * N], U8, align_bytes=64, name="wb")
        grouped = keep.tile([P, HALF, PACK], BF16, align_bytes=64, name="xb_grouped", tag="grouped_then_wa")
        codes = [keep.tile([P, HALF], U32, align_bytes=64, name=f"xb_codes{h}") for h in range(2)]
        scale = [keep.tile([P, HALF], U8, align_bytes=64, name=f"xb_scale{h}") for h in range(2)]
        for h in range(2):
            split = XB_VECTOR_COLS[h]
            interleave(nc.vector.tensor_copy, grouped[:, :split, :], xb_raw[h][:, :, :split])
            interleave(nc.scalar.copy, grouped[:, split:, :], xb_raw[h][:, :, split:])
            if h == 0:
                deal_columns(nc.vector, wb[:].bitcast(U16), wb_raw[:].bitcast(U16), 8)
            nc.vector.quantize_mx(
                out=codes[h][:].bitcast(FP8X4), scales=scale[h][:], in_=grouped[:].rearrange("p c j -> p (c j)")
            )
            if h == 0:
                deal_columns(nc.vector, wb_scale[:], wb_scale_raw[:], 16)
        wa = keep.tile([P, 2, N], I32, align_bytes=64, name="wa", tag="grouped_then_wa")
        for z in range(2):
            deal_columns(nc.vector, wa[:, z, :], wa_raw[:, z, :], 4)
        for h, r, i in ((0, 0, 4), (0, 1, 5), (1, 0, 6), (1, 1, 7), (0, 2, 6), (0, 3, 7), (1, 2, 4), (1, 3, 5)):
            acc = bank[i][:, :HALF]
            nc.tensor.matmul_mx(
                out=acc,
                lhsT=wb[:, 2 * P * r : 2 * P * (r + 1)].bitcast(FP4X4),
                lhsT_scale=wb_scale[:, P * r : P * (r + 1)],
                rhs=codes[h][:].bitcast(FP8X4),
                rhs_scale=scale[h][:],
                start=True,
                stop=True,
            )
            if (h, r) == (1, 0):
                nc.vector.tensor_scalar(zb[r][:, h * HALF : (h + 1) * HALF], acc, -1.0, None, ALU.mult)
            else:
                nc.scalar.activation(zb[r][:, h * HALF : (h + 1) * HALF], acc, ACT.Copy, scale=-1.0)

        wa_scale = keep.tile([P, 2, N], U8, align_bytes=64, name="wa_scale")
        for z in range(2):
            deal_columns(nc.vector, wa_scale[:, z, :], wa_scale_raw[:, z * N : (z + 1) * N], 16)
        b_all = keep.tile([P, PACK * T], F32, align_bytes=64, name="b_all", tag="later_b")
        b = [b_all[:, T * r : T * (r + 1)] for r in range(PACK)]
        for r in range(PACK):
            nc.vector.tensor_copy(b[r], zb[r].indirect(list_b[:]))
        for r in range(PACK):
            acc = bank[r]
            for z in range(2):
                nc.tensor.matmul_mx(
                    out=acc[:],
                    lhsT=wa[:, z, P * r : P * (r + 1)].bitcast(FP8X4),
                    lhsT_scale=wa_scale[:, z, P * r : P * (r + 1)],
                    rhs=xa[:, z, :].bitcast(FP4X4),
                    rhs_scale=xa_scale[:, z * I : (z + 1) * I],
                    start=(z == 0),
                    stop=(z == 1),
                )
            nc.scalar.copy(out=za[r][:, :I], in_=acc[:])

        y = keep.tile([P, PACK, T], F32, name="y")
        out_rows = out_0.rearrange("(p r) t -> p r t", r=PACK)
        scaled = keep.tile([P, TURNED, T], F32, name="scaled")
        nc.scalar.activation(scaled[:], res_pairs[0][:], ACT.Copy, scale=-0.3)

        def turn(acc, source, start, stop):
            for j in range(T // P):
                cols = slice(P * j, P * (j + 1))
                nc.tensor.matmul(
                    acc[:, cols],
                    source[:, cols],
                    ident[:],
                    start=start and j == 0,
                    stop=stop and j == T // P - 1,
                    is_transpose=True,
                )

        for r in range(TURNED):
            turn(bank[r], b[r], True, False)
            turn(bank[r], scaled[:, r, :], False, False)
        gaps, squares = [], []
        for r in range(PACK):
            gap = keep.tile([P, T], F32, name=f"gap{r}")
            nc.vector.tensor_tensor(gap[:], za[r][:].indirect(list_a[:]), b[r], ALU.add)
            square = keep.tile([P, T], F32, name=f"square{r}")
            nc.scalar.activation(square[:], gap[:], ACT.Square, scale=0.5)
            gaps.append(gap)
            squares.append(square)
            if r < TURNED:
                turn(bank[r], square, False, True)
                turned = keep.tile([P, T], F32, name=f"turned{r}")
                nc.scalar.copy(out=turned[:], in_=bank[r][:])
                turn(bank[PACK + r], turned, True, True)

        def store(r, cols):
            nc.sync.dma_start(out=out_rows[:, r, cols], in_=y[:, r, cols])

        bases = [b[r - TURNED] for r in range(TURNED, PACK)]
        largers = [keep.tile([P, T], F32, name=f"larger{r}") for r in range(TURNED, PACK)]
        for i, r in enumerate(range(TURNED, PACK)):
            nc.vector.scalar_tensor_tensor(bases[i], res_pairs[1][:, i, :], 0.3, b[r], ALU.mult, ALU.subtract)
        for i, r in enumerate(range(TURNED, PACK)):
            nc.vector.scalar_tensor_tensor(largers[i][:], gaps[r][:], 0.0, bases[i], ALU.max, ALU.add)
        for i, r in enumerate(range(TURNED, PACK)):
            nc.vector.tensor_tensor(y[:, r, :], largers[i][:], squares[r][:], ALU.subtract)
            store(r, slice(0, T))
        for r, cols in ((0, slice(0, T)), (1, slice(HALF, T)), (1, slice(0, HALF))):
            nc.vector.scalar_tensor_tensor(
                y[:, r, cols], gaps[r][:, cols], 0.0, bank[PACK + r][:, cols], ALU.max, ALU.subtract
            )
            store(r, cols)

        y_codes = keep.tile([P, T], U32, align_bytes=64, name="y_codes")
        y_scale = keep.tile([P, T], U8, align_bytes=64, name="y_scale")
        words_out = out_1[0].rearrange("p c t -> p (c t)").bitcast(I32)
        for h, copy in ((0, nc.vector.tensor_copy), (1, nc.scalar.copy)):
            cols = slice(h * HALF, (h + 1) * HALF)
            grouped_y = keep.tile([P, HALF, PACK], BF16, align_bytes=64, name=f"y_grouped{h}")
            interleave(copy, grouped_y[:], y[:, :, cols])
            nc.vector.quantize_mx(
                out=y_codes[:, cols].bitcast(FP8X4),
                scales=y_scale[:, cols],
                in_=grouped_y[:].rearrange("p c j -> p (c j)"),
            )
            nc.sync.dma_start(out=words_out[:, cols], in_=y_codes[:, cols].bitcast(I32))
        for q in range(4):
            queue = nc.scalar if q % 2 else nc.sync
            queue.dma_start(
                out=out_2[0, 4 * q : 4 * q + 4, :].bitcast(I32),
                in_=y_scale[32 * q : 32 * q + 4, :].bitcast(I32),
            )
